import numpy as np
import ml_dtypes


def mxq(x, axis, fmt="e4m3"):
    dtype, down = {"e4m3": (ml_dtypes.float8_e4m3fn, 7), "e5m2": (ml_dtypes.float8_e5m2, 14)}[fmt]
    v = np.moveaxis(np.asarray(x, np.float32).astype(ml_dtypes.bfloat16).astype(np.float64), axis, -1)
    blocks = v.reshape(v.shape[:-1] + (-1, 32))
    amax = np.abs(blocks).max(-1, keepdims=True)
    byte = np.maximum(np.where(amax > 0, np.frexp(amax)[1] - 1 + 127, 0) - down, 1)
    scale = np.exp2(byte - 127.0)
    codes = (blocks / scale).astype(np.float32).astype(dtype).astype(np.float64)
    return np.moveaxis((codes * scale).reshape(v.shape), -1, axis)


WIDE = False


def mx_kscale(k):
    if not WIDE:
        return np.ones(k)
    levels = np.array([10, -10, 5, -5, 0])
    if k % 512:
        return np.exp2(np.random.permutation(np.resize(levels, k // 32))).repeat(32)
    a = np.empty((k // 512, 16))
    for p in range(k // 512):
        a[p, :8] = np.random.permutation(np.resize(levels, 8))
        for g in range(8):
            far = levels[np.abs(levels - a[p, g]) >= 10]
            a[p, g + 8] = far[np.random.randint(len(far))]
    return np.exp2(a.ravel()).repeat(32)


BF16 = ml_dtypes.bfloat16


def bf(x):
    return np.asarray(x, np.float32).astype(BF16)


def f64(x):
    return np.asarray(x).astype(np.float64)


E2M1 = np.array([0.0, 0.5, 1.0, 1.5, 2.0, 3.0, 4.0, 6.0, -0.0, -0.5, -1.0, -1.5, -2.0, -3.0, -4.0, -6.0])


def pack_weight(w, fmt):
    k, n = w.shape
    w = f64(bf(w)).reshape(k // 32, 32, n)
    amax = np.abs(w).max(1)
    if fmt == "e4m3":
        byte = np.frexp(amax)[1] - 1 + 127 - 7
    else:
        mant, ex = np.frexp(amax / 6.0)
        byte = np.where(mant > 0.5, ex, ex - 1) + 127
    byte = np.clip(np.where(amax > 0, byte, 1), 1, 254)
    scaled = (w * np.exp2(127.0 - byte)[:, None, :]).reshape(k, n).astype(np.float32)
    by_word = np.ascontiguousarray(scaled.reshape(k // 512, 128, 4, n).transpose(0, 1, 3, 2))
    if fmt == "e4m3":
        words = by_word.astype(ml_dtypes.float8_e4m3fn).view(np.uint8)
    else:
        c = by_word.astype(ml_dtypes.float4_e2m1fn).view(np.uint8) & 0xF
        words = c[..., 0::2] | (c[..., 1::2] << 4)
    return np.ascontiguousarray(words), np.ascontiguousarray(byte.astype(np.uint8).reshape(k // 512, 16, n))


def unpack_weight(words, scales, fmt):
    g, p, n, _ = words.shape
    if fmt == "e4m3":
        vals = np.ascontiguousarray(words).view(ml_dtypes.float8_e4m3fn).astype(np.float64)
    else:
        nib = np.empty((g, p, n, 4), np.uint8)
        nib[..., 0::2] = words & 0xF
        nib[..., 1::2] = words >> 4
        vals = E2M1[nib]
    vals = vals * np.repeat(np.exp2(scales.astype(np.float64) - 127.0), 8, axis=1)[..., None]
    return vals.transpose(0, 1, 3, 2).reshape(g * 512, n)


I, J, K, S, R = 1024, 1024, 512, 1024, 1024

EPS = 1e-6


def column_rms_normalize(m):
    mean_sq = np.mean(m * m, axis=0, keepdims=True)
    return m / np.sqrt(mean_sq + EPS)


def draw0():
    sj, sk = mx_kscale(J), mx_kscale(K)
    u = mx_kscale(S)
    p = np.random.standard_normal((I, S)) * (0.08 / np.sqrt(S)) / u[None, :]
    p_words, p_scales = pack_weight(p.T, "e4m3")
    q_words, q_scales = pack_weight(np.random.standard_normal((J, S)) * (0.25 / np.sqrt(J)) * sj[:, None], "e4m3")
    t_words, t_scales = pack_weight(np.random.standard_normal((K, S)) * (0.25 / np.sqrt(K)) * sk[:, None], "e4m3")
    return {
        "p_words": p_words,
        "p_scales": p_scales,
        "q_words": q_words,
        "q_scales": q_scales,
        "t_words": t_words,
        "t_scales": t_scales,
        "mu": bf(np.random.uniform(0.5, 1.5, S) * u),
        "b": bf(np.random.standard_normal((J, R)) / sj[:, None]),
        "c": bf(np.random.standard_normal((K, R)) / sk[:, None]),
    }


def core(p_words, p_scales, q_words, q_scales, t_words, t_scales, mu, b, c):
    e = unpack_weight(q_words, q_scales, "e4m3").T @ mxq(f64(b), 0, "e4m3")
    f = unpack_weight(t_words, t_scales, "e4m3").T @ mxq(f64(c), 0, "e4m3")
    h = f64(mu)[:, None] * e * f
    m = unpack_weight(p_words, p_scales, "e4m3").T @ mxq(h, 0, "e4m3")
    return column_rms_normalize(m)


def e4m3fn_bytes(y):
    return np.clip(np.asarray(y, np.float64), -448.0, 448.0).astype(np.float32).astype(ml_dtypes.float8_e4m3fn).view(np.uint8)


def e4m3fn_values(b):
    return np.asarray(b, np.uint8).view(ml_dtypes.float8_e4m3fn).astype(np.float64)


def setup_inputs():
    d = draw0()
    x0 = np.asarray(d['b']).astype(np.float64)
    s = (np.max(np.abs(x0), axis=(1,), keepdims=True) / 448.0).astype(np.float32)
    out = {}
    for k, v in d.items():
        if k == 'b':
            out['b_bytes'] = e4m3fn_bytes(x0 / s.astype(np.float64))
            out['b_scale'] = s
        else:
            out[k] = v
    return out


def reference(p_words, p_scales, q_words, q_scales, t_words, t_scales, mu, b_bytes, b_scale, c):
    return core(p_words, p_scales, q_words, q_scales, t_words, t_scales, mu, e4m3fn_values(b_bytes) * b_scale.astype(np.float64), c)

@@ -1,0 +1,354 @@
+from contextlib import ExitStack
+
+import concourse.mybir as mybir
+from concourse.masks import make_identity
+
+I, J, K, S, R = 1024, 1024, 512, 1024, 1024
+EPS = 1e-6
+FLOPS = 2 * S * R * (J + K + I)
+
+F32 = mybir.dt.float32
+BF16 = mybir.dt.bfloat16
+U32 = mybir.dt.uint32
+I32 = mybir.dt.int32
+U8 = mybir.dt.uint8
+FP8 = mybir.dt.float8_e4m3fn
+FP8X4 = mybir.dt.float8_e4m3fn_x4
+ACT = mybir.ActivationFunctionType
+ALU = mybir.AluOpType
+
+P = 128
+PACK = 4
+BANK = 512
+WIDTHS = (128, 256, 256, 256, 128)
+RUN = 4
+EARLY = 4
+TAIL = 2
+LAG = {'wid': -250, 'mc': -224, 'qc': -200, 'mu': -278, 'w0': -94, 'w1': 10, 'mb': -160, 'qb': -130, 'f': 0, 'e': 100, 'qh': 150, 'mt': 350, 'n': 380, 'm': 640}
+B_LOADS = ([0], [1, 2], [3, 4])
+
+
+def weave(main, fillers):
+    done = 0
+    if len(main) == 0:
+        main = [lambda: None]
+    for n, step in enumerate(main):
+        step()
+        upto = min(len(fillers), -(-(n + 1) * len(fillers) // len(main)))
+        for filler in fillers[done:upto]:
+            filler()
+        done = upto
+
+
+def zipped(first, second):
+    steps = []
+    for n in range(max(len(first), len(second))):
+        steps.extend(first[n : n + 1])
+        steps.extend(second[n : n + 1])
+    return steps
+
+
+def tile_cptensorsimultaneouspowerstep_w8_kernel(
+    tc, p_words, p_scales, q_words, q_scales, t_words, t_scales, mu, b_bytes, b_scale, c, out
+):
+    nc = tc.nc
+    chunks = len(WIDTHS)
+    starts = [sum(WIDTHS[:k]) for k in range(chunks)]
+
+    with ExitStack() as ctx:
+        keep = ctx.enter_context(tc.tile_pool(name="keep", bufs=1))
+        stage = ctx.enter_context(tc.tile_pool(name="stage", bufs=3))
+        psum = ctx.enter_context(tc.psum_pool(name="psum", bufs=8))
+        ctx.enter_context(tc.manual_schedule())
+
+        def kept(name, shape, dtype):
+            return keep.tile(shape, dtype, name=name, align_bytes=64)
+
+        def bank(name):
+            return psum.tile([P, BANK], F32, name=name, tag="bank")
+
+        qt_scale_raw = kept("qt_scale_raw", [P, S], U8)
+        p_scale = kept("p_scale", [P, I], U8)
+        nc.vector.memset(qt_scale_raw[:].bitcast(I32), 0)
+        nc.vector.memset(p_scale[:].bitcast(I32), 0)
+        warm = kept("warm", [P, 8], F32)
+        nc.vector.memset(warm[:], 1.0)
+        nc.scalar.activation(out=warm[:, 4:5], in_=warm[:, 0:1], func=ACT.Abs_reciprocal_sqrt)
+
+        def load_scales(engine, tile, row0, scales):
+            groups = scales.shape[0]
+            for quad in range(4):
+                first = 32 * quad + row0
+                engine.dma_start(
+                    out=tile[first : first + 4 * groups, :].bitcast(I32),
+                    in_=scales[:, 4 * quad : 4 * quad + 4, :].bitcast(I32),
+                )
+
+        c_rows = c.rearrange("(p t) r -> p t r", t=PACK)
+        b_rows = b_bytes.rearrange("(g p t) r -> g p t r", p=P, t=PACK)
+        c_raw, b_raw = {}, {}
+
+        def load_c(ks):
+            r0, r1 = starts[ks[0]], starts[ks[-1]] + WIDTHS[ks[-1]]
+            tile = kept("c_raw%d" % ks[0], [P, PACK, r1 - r0], BF16)
+            nc.sync.dma_start(out=tile[:], in_=c_rows[:, :, r0:r1])
+            for k in ks:
+                c_raw[k] = tile[:, :, starts[k] - r0 : starts[k] - r0 + WIDTHS[k]]
+
+        def load_b(ks):
+            r0, r1 = starts[ks[0]], starts[ks[-1]] + WIDTHS[ks[-1]]
+            for g in range(2):
+                tile = kept("b_raw%d_%d" % (ks[0], g), [P, PACK, r1 - r0], U8)
+                nc.sync.dma_start(out=tile[:], in_=b_rows[g][:, :, r0:r1])
+                for k in ks:
+                    b_raw[k, g] = tile[:, :, starts[k] - r0 : starts[k] - r0 + WIDTHS[k]]
+
+        def load_words(name, words, n0, n1):
+            groups = words.shape[0]
+            tile = kept(name, [P, groups, n1 - n0], U32)
+            nc.sync.dma_start(
+                out=tile[:].bitcast(I32),
+                in_=words.rearrange("g p n t -> p g (n t)")[:, :, PACK * n0 : PACK * n1].bitcast(I32),
+            )
+            return tile
+
+        b_scale_sb = kept("b_scale_sb", [P, 2, PACK], F32)
+        mu_raw = kept("mu_raw", [P, 2, PACK], BF16)
+        t_raw, q_raw = {}, {}
+
+        load_scales(nc.gpsimd, qt_scale_raw, 8, t_scales)
+        ident = kept("ident", [P, P], F32)
+        make_identity(nc, ident[:])
+        p_code = {}
+        nc.sync.dma_start(out=b_scale_sb[:], in_=b_scale.rearrange("(g p t) o -> p g (t o)", p=P, t=PACK))
+        load_c([0])
+        load_b([0])
+        t_raw[0] = load_words("t_raw0", t_words, 0, 512)
+        q_raw[0] = load_words("q_raw0", q_words, 0, 512)
+        load_scales(nc.sync, qt_scale_raw, 0, q_scales)
+        nc.sync.dma_start(out=mu_raw[:], in_=mu.rearrange("(g p t) -> p g t", p=P, t=PACK))
+        t_raw[1] = load_words("t_raw1", t_words, 512, 1024)
+        q_raw[1] = load_words("q_raw1", q_words, 512, 1024)
+        load_c([1])
+        load_b([1])
+        p_code[0] = load_words("p_code0", p_words, 0, 512)
+        load_scales(nc.sync, p_scale, 0, p_scales)
+        p_code[1] = load_words("p_code1", p_words, 512, 1024)
+        load_c([2])
+        load_b(list(range(2, chunks)))
+        load_c(list(range(3, chunks)))
+
+        mu_f32 = kept("mu_f32", [P, 2, PACK], F32)
+        t_code, q_code, qt_scale = {}, {}, {}
+
+        def permute_words(dst, src, name, half):
+            groups = src[half].shape[1]
+            dst[half] = kept("%s%d" % (name, half), [P, groups, PACK, P], U32)
+            nc.vector.tensor_copy(
+                out=dst[half][:].bitcast(I32).rearrange("p g t m -> p g m t"),
+                in_=src[half][:].bitcast(I32).rearrange("p g (m t) -> p g m t", t=PACK),
+            )
+
+        def permute_scales(half):
+            qt_scale[half] = kept("qt_scale%d" % half, [P, PACK, P], U8)
+            nc.vector.tensor_copy(
+                out=qt_scale[half][:],
+                in_=qt_scale_raw[:, 512 * half : 512 * (half + 1)].rearrange("p (m t) -> p t m", t=PACK),
+            )
+
+        b_wide, b_mixed, c_mixed, f_sb, h_mixed = {}, {}, {}, {}, {}
+        b_code, b_sc, c_code, c_sc, h_code, h_sc = {}, {}, {}, {}, {}, {}
+        ssq, rnorm = {}, {}
+
+        def widen_b(k, g, t):
+            if t == 0:
+                b_wide[k, g] = stage.tile([P, PACK, WIDTHS[k]], BF16, name="b_wide%d_%d" % (k, g), tag="b_wide", bufs=6)
+            nc.scalar.activation(
+                out=b_wide[k, g][:, t, :], in_=b_raw[k, g][:, t, :].bitcast(FP8), func=ACT.Copy,
+                scale=b_scale_sb[:, g, t : t + 1],
+            )
+
+        def interleave(dst, src):
+            nc.vector.tensor_copy(
+                out=dst.rearrange("p (c i) t -> p c t i", i=RUN),
+                in_=src.rearrange("p t (c i) -> p c t i", i=RUN),
+            )
+
+        def mix_b(k, g):
+            if g == 0:
+                b_mixed[k] = stage.tile([P, 2, WIDTHS[k], PACK], BF16, name="b_mixed%d" % k, tag="b_mixed", align_bytes=64, bufs=3)
+            interleave(b_mixed[k][:, g], b_wide[k, g][:])
+
+        def mix_c(k):
+            c_mixed[k] = stage.tile([P, WIDTHS[k], PACK], BF16, name="c_mixed%d" % k, tag="c_mixed", align_bytes=64, bufs=3)
+            interleave(c_mixed[k][:], c_raw[k])
+
+        def quantize(name, codes, scales, key, width, src):
+            codes[key] = kept(name + "_code", [P, width], U32)
+            scales[key] = kept(name + "_sc", [P, width], U8)
+            nc.vector.quantize_mx(out=codes[key][:].bitcast(FP8X4), scales=scales[key][:], in_=src)
+
+        def quant_b(k):
+            quantize("b%d" % k, b_code, b_sc, k, 2 * WIDTHS[k], b_mixed[k][:].rearrange("p g r t -> p (g r t)"))
+
+        def quant_c(k):
+            quantize("c%d" % k, c_code, c_sc, k, WIDTHS[k], c_mixed[k][:].rearrange("p r t -> p (r t)"))
+
+        def quant_h(k, half):
+            quantize("h%d_%d" % (k, half), h_code, h_sc, (k, half), WIDTHS[k],
+                     h_mixed[k, half][:].rearrange("p r t -> p (r t)"))
+
+        def f_bank(k, half, t0):
+            w = WIDTHS[k]
+            if t0 == 0:
+                f_sb[k, half] = stage.tile([P, PACK, w], F32, name="f_sb%d_%d" % (k, half), tag="f_sb", bufs=6)
+            acc = bank("f_acc%d_%d_%d" % (k, half, t0))
+            slots = range(t0, t0 + BANK // w)
+            for t in slots:
+                nc.tensor.matmul_mx(
+                    out=acc[:, (t - t0) * w : (t - t0 + 1) * w],
+                    lhsT=t_code[half][:, 0, t, :].bitcast(FP8X4), lhsT_scale=qt_scale[half][8:P, t, :],
+                    rhs=c_code[k][:].bitcast(FP8X4), rhs_scale=c_sc[k][:], start=True, stop=True,
+                )
+            for t in slots:
+                nc.scalar.activation(
+                    out=f_sb[k, half][:, t, :], in_=acc[:, (t - t0) * w : (t - t0 + 1) * w], func=ACT.Copy,
+                    scale=mu_f32[:, half, t : t + 1],
+                )
+
+        def e_bank(k, half, rt):
+            w = WIDTHS[k]
+            if rt == 0:
+                h_mixed[k, half] = stage.tile([P, w, PACK], BF16, name="h_mixed%d_%d" % (k, half), tag="h_mixed", align_bytes=64, bufs=6)
+            acc = bank("e_acc%d_%d_%d" % (k, half, rt))
+            for t in range(PACK):
+                for g in range(2):
+                    cols = slice(g * w + rt * P, g * w + (rt + 1) * P)
+                    nc.tensor.matmul_mx(
+                        out=acc[:, t * P : (t + 1) * P],
+                        lhsT=q_code[half][:, g, t, :].bitcast(FP8X4), lhsT_scale=qt_scale[half][4 * g : P, t, :],
+                        rhs=b_code[k][:, cols].bitcast(FP8X4), rhs_scale=b_sc[k][:, cols],
+                        start=(g == 0), stop=(g == 1),
+                    )
+            cols = slice(rt * P, (rt + 1) * P)
+            nc.vector.tensor_tensor(
+                out=h_mixed[k, half][:, cols, :].rearrange("p (c i) t -> p c t i", i=RUN),
+                in0=acc[:].rearrange("p (t c i) -> p c t i", t=PACK, i=RUN),
+                in1=f_sb[k, half][:, :, cols].rearrange("p t (c i) -> p c t i", i=RUN),
+                op=ALU.mult,
+            )
+
+        def mt_bank(k, rt, ih):
+            if rt == 0 and ih == 0:
+                ssq[k] = kept("ssq%d" % k, [P, 2 * WIDTHS[k] // P], F32)
+            acc = bank("mt_acc%d_%d_%d" % (k, rt, ih))
+            cols, rows = slice(rt * P, (rt + 1) * P), slice(ih * BANK, (ih + 1) * BANK)
+            for half in range(2):
+                nc.tensor.matmul_mx(
+                    out=acc[:],
+                    lhsT=h_code[k, half][:, cols].bitcast(FP8X4), lhsT_scale=h_sc[k, half][:, cols],
+                    rhs=p_code[ih][:, half, :].bitcast(FP8X4), rhs_scale=p_scale[4 * half : P, rows],
+                    start=(half == 0), stop=(half == 1),
+                )
+            squares = stage.tile([P, BANK], F32, name="squares%d_%d_%d" % (k, rt, ih), tag="squares")
+            nc.scalar.activation(out=squares[:], in_=acc[:], func=ACT.Square,
+                                 accum_out=ssq[k][:, 2 * rt + ih : 2 * rt + ih + 1])
+
+        def spread_norm(k):
+            w = WIDTHS[k]
+            acc = bank("ssq_acc%d" % k)
+            for rt in range(w // P):
+                for ih in range(2):
+                    col = 2 * rt + ih
+                    nc.tensor.matmul(
+                        out=acc[:, rt * P : (rt + 1) * P],
+                        lhsT=ssq[k][:, col : col + 1].to_broadcast([P, P]), rhs=ident[:],
+                        start=(ih == 0), stop=(ih == 1), is_transpose=True,
+                    )
+            rnorm[k] = kept("rnorm%d" % k, [P, w], F32)
+            nc.scalar.activation(out=rnorm[k][:], in_=acc[:, 0:w], func=ACT.Abs_reciprocal_sqrt,
+                                 scale=1.0 / I, bias=EPS)
+
+        out_rows = out.rearrange("(a p) r -> p a r", p=P)
+
+        def m_bank(k, a0):
+            w = WIDTHS[k]
+            tiles = BANK // w
+            acc = bank("m_acc%d_%d" % (k, a0))
+            for a in range(a0, a0 + tiles):
+                rows = slice(a * P, (a + 1) * P)
+                for half in range(2):
+                    nc.tensor.matmul_mx(
+                        out=acc[:, (a - a0) * w : (a - a0 + 1) * w],
+                        lhsT=p_code[a // 4][:, half, (a % 4) * P : (a % 4 + 1) * P].bitcast(FP8X4), lhsT_scale=p_scale[4 * half : P, rows],
+                        rhs=h_code[k, half][:].bitcast(FP8X4), rhs_scale=h_sc[k, half][:],
+                        start=(half == 0), stop=(half == 1),
+                    )
+            result = stage.tile([P, tiles, w], F32, name="result%d_%d" % (k, a0), tag="result", bufs=8)
+            nc.vector.tensor_tensor(
+                out=result[:], in0=acc[:].rearrange("p (a r) -> p a r", a=tiles),
+                in1=rnorm[k][:].unsqueeze(1).to_broadcast([P, tiles, w]), op=ALU.mult,
+            )
+            nc.sync.dma_start(out=out_rows[:, a0 : a0 + tiles, starts[k] : starts[k] + w], in_=result[:])
+
+        def steps(fn, k, *ranges):
+            if k < 0 or k >= chunks:
+                return []
+            w = WIDTHS[k]
+            args = [()]
+            for rng in ranges:
+                args = [a + (x,) for a in args for x in rng(w)]
+            return [(lambda a=a: fn(k, *a)) for a in args]
+
+        two = lambda w: range(2)
+        four = lambda w: range(PACK)
+        r_tiles = lambda w: range(w // P)
+        t_starts = lambda w: range(0, PACK, BANK // w)
+        a_starts = lambda w: range(0, I // P, BANK // w)
+
+        def run(todo):
+            for step in todo:
+                step()
+
+        run(steps(widen_b, 0, two, four))
+        mix_c(0)
+        quant_c(0)
+        mix_b(0, 0)
+        permute_words(t_code, t_raw, "t_code", 0)
+        mix_b(0, 1)
+        permute_scales(0)
+        nc.vector.tensor_copy(out=mu_f32[:], in_=mu_raw[:])
+        quant_b(0)
+        permute_words(q_code, q_raw, "q_code", 0)
+        permute_words(t_code, t_raw, "t_code", 1)
+        permute_scales(1)
+        permute_words(q_code, q_raw, "q_code", 1)
+        for k in range(-1, chunks - 2):
+            run(steps(f_bank, k + 1, two, t_starts))
+            run(steps(mt_bank, k, r_tiles, two))
+            wide = steps(widen_b, k + 2, two, four)
+            run(wide[:EARLY])
+            if k < 0:
+                weave(steps(e_bank, 0, two, r_tiles), steps(mix_c, 1) + steps(quant_c, 1))
+            else:
+                run(steps(e_bank, k + 1, two, r_tiles))
+            run(steps(spread_norm, k))
+            run(wide[EARLY:])
+            run(steps(quant_h, k + 1, two))
+            mix = steps(mix_b, k + 2, two)
+            run(mix[:1])
+            weave(steps(m_bank, k, a_starts), mix[1:] + steps(quant_b, k + 2) + steps(mix_c, k + 3) + steps(quant_c, k + 3))
+        k = chunks - 2
+        mt = steps(mt_bank, k, r_tiles, two)
+        m = steps(m_bank, k, a_starts)
+        run(steps(f_bank, k + 1, two, t_starts))
+        run(mt[:2])
+        run(steps(e_bank, k + 1, two, r_tiles))
+        run(mt[2:])
+        run(steps(quant_h, k + 1, two))
+        run(steps(mt_bank, k + 1, r_tiles, two))
+        run(steps(spread_norm, k))
+        run(m[:TAIL])
+        run(steps(spread_norm, k + 1))
+        run(m[TAIL:])
+        run(steps(m_bank, k + 1, a_starts))

@@ -24,6 +24,11 @@ WIDTHS = (128, 256, 256, 256, 128)
 RUN = 4
 EARLY = 4
 TAIL = 2
+T1 = 1
+T2 = 2
+C_ON_S = (1,)
+LOADS = "bs b01 c0 ts t0 q0 qs mu t1 q1 c1 p0 ps p1 c2 b2 c3"
+HEAD = "w0 mc0 qc0 mb00 pt0 mb01 ps0 mu qb0 w10 pq0 f00 pt1 ps1 e00 w11 f01 mc1 pq1 mb10 e01 qc1 mb11 f10 qh0 qh1 f11 qb1 mc2 qc2"
 LAG = {'wid': -250, 'mc': -224, 'qc': -200, 'mu': -278, 'w0': -94, 'w1': 10, 'mb': -160, 'qb': -130, 'f': 0, 'e': 100, 'qh': 150, 'mt': 350, 'n': 380, 'm': 640}
 B_LOADS = ([0], [1, 2], [3, 4])
 
@@ -116,27 +121,27 @@ def tile_cptensorsimultaneouspowerstep_w8_kernel(
         mu_raw = kept("mu_raw", [P, 2, PACK], BF16)
         t_raw, q_raw = {}, {}
 
-        load_scales(nc.gpsimd, qt_scale_raw, 8, t_scales)
         ident = kept("ident", [P, P], F32)
         make_identity(nc, ident[:])
         p_code = {}
-        nc.sync.dma_start(out=b_scale_sb[:], in_=b_scale.rearrange("(g p t) o -> p g (t o)", p=P, t=PACK))
-        load_c([0])
-        load_b([0])
-        t_raw[0] = load_words("t_raw0", t_words, 0, 512)
-        q_raw[0] = load_words("q_raw0", q_words, 0, 512)
-        load_scales(nc.sync, qt_scale_raw, 0, q_scales)
-        nc.sync.dma_start(out=mu_raw[:], in_=mu.rearrange("(g p t) -> p g t", p=P, t=PACK))
-        t_raw[1] = load_words("t_raw1", t_words, 512, 1024)
-        q_raw[1] = load_words("q_raw1", q_words, 512, 1024)
-        load_c([1])
-        load_b([1])
-        p_code[0] = load_words("p_code0", p_words, 0, 512)
-        load_scales(nc.sync, p_scale, 0, p_scales)
-        p_code[1] = load_words("p_code1", p_words, 512, 1024)
-        load_c([2])
-        load_b(list(range(2, chunks)))
-        load_c(list(range(3, chunks)))
+        rest = list(range(2, chunks))
+        loads = {
+            "bs": lambda: nc.sync.dma_start(out=b_scale_sb[:], in_=b_scale.rearrange("(g p t) o -> p g (t o)", p=P, t=PACK)),
+            "mu": lambda: nc.sync.dma_start(out=mu_raw[:], in_=mu.rearrange("(g p t) -> p g t", p=P, t=PACK)),
+            "c0": lambda: load_c([0]), "c1": lambda: load_c([1]), "c01": lambda: load_c([0, 1]), "c2": lambda: load_c([2]), "c3": lambda: load_c(rest[1:]),
+            "b0": lambda: load_b([0]), "b1": lambda: load_b([1]), "b01": lambda: load_b([0, 1]), "b2": lambda: load_b(rest),
+            "t0": lambda: t_raw.setdefault(0, load_words("t_raw0", t_words, 0, 512)),
+            "t1": lambda: t_raw.setdefault(1, load_words("t_raw1", t_words, 512, 1024)),
+            "q0": lambda: q_raw.setdefault(0, load_words("q_raw0", q_words, 0, 512)),
+            "q1": lambda: q_raw.setdefault(1, load_words("q_raw1", q_words, 512, 1024)),
+            "p0": lambda: p_code.setdefault(0, load_words("p_code0", p_words, 0, 512)),
+            "p1": lambda: p_code.setdefault(1, load_words("p_code1", p_words, 512, 1024)),
+            "qs": lambda: load_scales(nc.sync, qt_scale_raw, 0, q_scales),
+            "ts": lambda: load_scales(nc.sync, qt_scale_raw, 8, t_scales),
+            "ps": lambda: load_scales(nc.sync, p_scale, 0, p_scales),
+        }
+        for name in LOADS.split():
+            loads[name]()
 
         mu_f32 = kept("mu_f32", [P, 2, PACK], F32)
         t_code, q_code, qt_scale = {}, {}, {}
@@ -145,8 +150,8 @@ def tile_cptensorsimultaneouspowerstep_w8_kernel(
             groups = src[half].shape[1]
             dst[half] = kept("%s%d" % (name, half), [P, groups, PACK, P], U32)
             nc.vector.tensor_copy(
-                out=dst[half][:].bitcast(I32).rearrange("p g t m -> p g m t"),
-                in_=src[half][:].bitcast(I32).rearrange("p g (m t) -> p g m t", t=PACK),
+                out=dst[half][:].bitcast(I32).rearrange("p g t (c i) -> p g c t i", i=PACK),
+                in_=src[half][:].bitcast(I32).rearrange("p g (c i t) -> p g c t i", i=PACK, t=PACK),
             )
 
         def permute_scales(half):
@@ -168,8 +173,8 @@ def tile_cptensorsimultaneouspowerstep_w8_kernel(
                 scale=b_scale_sb[:, g, t : t + 1],
             )
 
-        def interleave(dst, src):
-            nc.vector.tensor_copy(
+        def interleave(dst, src, copy=nc.vector.tensor_copy):
+            copy(
                 out=dst.rearrange("p (c i) t -> p c t i", i=RUN),
                 in_=src.rearrange("p t (c i) -> p c t i", i=RUN),
             )
@@ -181,7 +186,7 @@ def tile_cptensorsimultaneouspowerstep_w8_kernel(
 
         def mix_c(k):
             c_mixed[k] = stage.tile([P, WIDTHS[k], PACK], BF16, name="c_mixed%d" % k, tag="c_mixed", align_bytes=64, bufs=3)
-            interleave(c_mixed[k][:], c_raw[k])
+            interleave(c_mixed[k][:], c_raw[k], nc.scalar.copy if k in C_ON_S else nc.vector.tensor_copy)
 
         def quantize(name, codes, scales, key, width, src):
             codes[key] = kept(name + "_code", [P, width], U32)
@@ -232,9 +237,9 @@ def tile_cptensorsimultaneouspowerstep_w8_kernel(
                     )
             cols = slice(rt * P, (rt + 1) * P)
             nc.vector.tensor_tensor(
-                out=h_mixed[k, half][:, cols, :].rearrange("p (c i) t -> p c t i", i=RUN),
-                in0=acc[:].rearrange("p (t c i) -> p c t i", t=PACK, i=RUN),
-                in1=f_sb[k, half][:, :, cols].rearrange("p t (c i) -> p c t i", i=RUN),
+                out=h_mixed[k, half][:, cols, :].rearrange("p (c i) t -> p c t i", i=2),
+                in0=acc[:].rearrange("p (t c i) -> p c t i", t=PACK, i=2),
+                in1=f_sb[k, half][:, :, cols].rearrange("p t (c i) -> p c t i", i=2),
                 op=ALU.mult,
             )
 
@@ -310,44 +315,44 @@ def tile_cptensorsimultaneouspowerstep_w8_kernel(
             for step in todo:
                 step()
 
-        run(steps(widen_b, 0, two, four))
-        mix_c(0)
-        quant_c(0)
-        mix_b(0, 0)
-        permute_words(t_code, t_raw, "t_code", 0)
-        mix_b(0, 1)
-        permute_scales(0)
-        nc.vector.tensor_copy(out=mu_f32[:], in_=mu_raw[:])
-        quant_b(0)
-        permute_words(q_code, q_raw, "q_code", 0)
-        permute_words(t_code, t_raw, "t_code", 1)
-        permute_scales(1)
-        permute_words(q_code, q_raw, "q_code", 1)
-        for k in range(-1, chunks - 2):
-            run(steps(f_bank, k + 1, two, t_starts))
+        wide = steps(widen_b, 1, two, four)
+        f1 = steps(f_bank, 1, two, t_starts)
+        head = {
+            "w0": lambda: run(steps(widen_b, 0, two, four)), "w10": lambda: run(wide[:4]), "w11": lambda: run(wide[4:]),
+            "mc0": lambda: mix_c(0), "mc1": lambda: mix_c(1), "mc2": lambda: mix_c(2),
+            "qc0": lambda: quant_c(0), "qc1": lambda: quant_c(1), "qc2": lambda: quant_c(2),
+            "mb00": lambda: mix_b(0, 0), "mb01": lambda: mix_b(0, 1), "mb10": lambda: mix_b(1, 0), "mb11": lambda: mix_b(1, 1),
+            "qb0": lambda: quant_b(0), "qb1": lambda: quant_b(1),
+            "pt0": lambda: permute_words(t_code, t_raw, "t_code", 0), "pt1": lambda: permute_words(t_code, t_raw, "t_code", 1),
+            "pq0": lambda: permute_words(q_code, q_raw, "q_code", 0), "pq1": lambda: permute_words(q_code, q_raw, "q_code", 1),
+            "ps0": lambda: permute_scales(0), "ps1": lambda: permute_scales(1),
+            "mu": lambda: nc.vector.tensor_copy(out=mu_f32[:], in_=mu_raw[:]),
+            "f00": lambda: f_bank(0, 0, 0), "f01": lambda: f_bank(0, 1, 0), "e00": lambda: e_bank(0, 0, 0), "e01": lambda: e_bank(0, 1, 0),
+            "f10": lambda: run(f1[: len(f1) // 2]), "f11": lambda: run(f1[len(f1) // 2 :]),
+            "qh0": lambda: quant_h(0, 0), "qh1": lambda: quant_h(0, 1),
+        }
+        for name in HEAD.split():
+            head[name]()
+        for k in range(chunks - 2):
             run(steps(mt_bank, k, r_tiles, two))
-            wide = steps(widen_b, k + 2, two, four)
-            run(wide[:EARLY])
-            if k < 0:
-                weave(steps(e_bank, 0, two, r_tiles), steps(mix_c, 1) + steps(quant_c, 1))
-            else:
-                run(steps(e_bank, k + 1, two, r_tiles))
+            run(steps(widen_b, k + 2, two, four))
+            run(steps(e_bank, k + 1, two, r_tiles))
             run(steps(spread_norm, k))
-            run(wide[EARLY:])
+            run(steps(f_bank, k + 2, two, t_starts))
             run(steps(quant_h, k + 1, two))
-            mix = steps(mix_b, k + 2, two)
-            run(mix[:1])
-            weave(steps(m_bank, k, a_starts), mix[1:] + steps(quant_b, k + 2) + steps(mix_c, k + 3) + steps(quant_c, k + 3))
+            run(steps(mix_b, k + 2, two))
+            weave(steps(m_bank, k, a_starts), steps(quant_b, k + 2) + steps(mix_c, k + 3) + steps(quant_c, k + 3))
         k = chunks - 2
         mt = steps(mt_bank, k, r_tiles, two)
         m = steps(m_bank, k, a_starts)
-        run(steps(f_bank, k + 1, two, t_starts))
-        run(mt[:2])
+        run(mt[:T1])
         run(steps(e_bank, k + 1, two, r_tiles))
-        run(mt[2:])
+        run(mt[T1:])
         run(steps(quant_h, k + 1, two))
-        run(steps(mt_bank, k + 1, r_tiles, two))
+        mt = steps(mt_bank, k + 1, r_tiles, two)
+        run(mt[:T2])
         run(steps(spread_norm, k))
+        run(mt[T2:])
         run(m[:TAIL])
         run(steps(spread_norm, k + 1))
         run(m[TAIL:])

@@ -27,8 +27,8 @@ TAIL = 2
 T1 = 1
 T2 = 2
 C_ON_S = (1,)
-LOADS = "bs b01 c0 ts t0 q0 qs mu t1 q1 c1 p0 ps p1 c2 b2 c3"
-HEAD = "w0 mc0 qc0 mb00 pt0 mb01 ps0 mu qb0 w10 pq0 f00 pt1 ps1 e00 w11 f01 mc1 pq1 mb10 e01 qc1 mb11 f10 qh0 qh1 f11 qb1 mc2 qc2"
+LOADS = "id bs c0 b01 ts t0 q0 c1 qs mu t1 q1 p0 ps p1 c2 b2 c3"
+HEAD = "w00 w01 mc0 qc0 mb00 mb01 pt0 w10 w11 qb0 pq0 ps0 ps1 mu0 pt1 mc1 f000 f010 mb10 pq1 qc1 e000 mb11 e010 f100 f102 f110 f112 qb1 qh00 qh01 mc2 qc2 mt000 mt001 w20 w21 e100 e101 e110 e111 n0 f200 f202 f210 f212 qh10 qh11 mb20 mb21 m00 qb2 mc3 m04 qc3"
 LAG = {'wid': -250, 'mc': -224, 'qc': -200, 'mu': -278, 'w0': -94, 'w1': 10, 'mb': -160, 'qb': -130, 'f': 0, 'e': 100, 'qh': 150, 'mt': 350, 'n': 380, 'm': 640}
 B_LOADS = ([0], [1, 2], [3, 4])
 
@@ -122,7 +122,6 @@ def tile_cptensorsimultaneouspowerstep_w8_kernel(
         t_raw, q_raw = {}, {}
 
         ident = kept("ident", [P, P], F32)
-        make_identity(nc, ident[:])
         p_code = {}
         rest = list(range(2, chunks))
         loads = {
@@ -138,6 +137,10 @@ def tile_cptensorsimultaneouspowerstep_w8_kernel(
             "p1": lambda: p_code.setdefault(1, load_words("p_code1", p_words, 512, 1024)),
             "qs": lambda: load_scales(nc.sync, qt_scale_raw, 0, q_scales),
             "ts": lambda: load_scales(nc.sync, qt_scale_raw, 8, t_scales),
+            "tsG": lambda: load_scales(nc.gpsimd, qt_scale_raw, 8, t_scales),
+            "psG": lambda: load_scales(nc.gpsimd, p_scale, 0, p_scales),
+            "muG": lambda: nc.gpsimd.dma_start(out=mu_raw[:], in_=mu.rearrange("(g p t) -> p g t", p=P, t=PACK)),
+            "id": lambda: make_identity(nc, ident[:]),
             "ps": lambda: load_scales(nc.sync, p_scale, 0, p_scales),
         }
         for name in LOADS.split():
@@ -179,10 +182,10 @@ def tile_cptensorsimultaneouspowerstep_w8_kernel(
                 in_=src.rearrange("p t (c i) -> p c t i", i=RUN),
             )
 
-        def mix_b(k, g):
-            if g == 0:
+        def mix_b(k, g, copy=nc.vector.tensor_copy):
+            if k not in b_mixed:
                 b_mixed[k] = stage.tile([P, 2, WIDTHS[k], PACK], BF16, name="b_mixed%d" % k, tag="b_mixed", align_bytes=64, bufs=3)
-            interleave(b_mixed[k][:, g], b_wide[k, g][:])
+            interleave(b_mixed[k][:, g], b_wide[k, g][:], copy)
 
         def mix_c(k):
             c_mixed[k] = stage.tile([P, WIDTHS[k], PACK], BF16, name="c_mixed%d" % k, tag="c_mixed", align_bytes=64, bufs=3)
@@ -205,7 +208,7 @@ def tile_cptensorsimultaneouspowerstep_w8_kernel(
 
         def f_bank(k, half, t0):
             w = WIDTHS[k]
-            if t0 == 0:
+            if (k, half) not in f_sb:
                 f_sb[k, half] = stage.tile([P, PACK, w], F32, name="f_sb%d_%d" % (k, half), tag="f_sb", bufs=6)
             acc = bank("f_acc%d_%d_%d" % (k, half, t0))
             slots = range(t0, t0 + BANK // w)
@@ -223,7 +226,7 @@ def tile_cptensorsimultaneouspowerstep_w8_kernel(
 
         def e_bank(k, half, rt):
             w = WIDTHS[k]
-            if rt == 0:
+            if (k, half) not in h_mixed:
                 h_mixed[k, half] = stage.tile([P, w, PACK], BF16, name="h_mixed%d_%d" % (k, half), tag="h_mixed", align_bytes=64, bufs=6)
             acc = bank("e_acc%d_%d_%d" % (k, half, rt))
             for t in range(PACK):
@@ -244,7 +247,7 @@ def tile_cptensorsimultaneouspowerstep_w8_kernel(
             )
 
         def mt_bank(k, rt, ih):
-            if rt == 0 and ih == 0:
+            if k not in ssq:
                 ssq[k] = kept("ssq%d" % k, [P, 2 * WIDTHS[k] // P], F32)
             acc = bank("mt_acc%d_%d_%d" % (k, rt, ih))
             cols, rows = slice(rt * P, (rt + 1) * P), slice(ih * BANK, (ih + 1) * BANK)
@@ -296,6 +299,12 @@ def tile_cptensorsimultaneouspowerstep_w8_kernel(
             )
             nc.sync.dma_start(out=out_rows[:, a0 : a0 + tiles, starts[k] : starts[k] + w], in_=result[:])
 
+        def warm_pe(count):
+            acc = bank("warm_acc")
+            src = c_mixed[0][:].rearrange("p r t -> p (r t)")
+            for n in range(count):
+                nc.tensor.matmul(out=acc[:], lhsT=src[:, 0:P], rhs=src, start=True, stop=True)
+
         def steps(fn, k, *ranges):
             if k < 0 or k >= chunks:
                 return []
@@ -315,25 +324,16 @@ def tile_cptensorsimultaneouspowerstep_w8_kernel(
             for step in todo:
                 step()
 
-        wide = steps(widen_b, 1, two, four)
-        f1 = steps(f_bank, 1, two, t_starts)
-        head = {
-            "w0": lambda: run(steps(widen_b, 0, two, four)), "w10": lambda: run(wide[:4]), "w11": lambda: run(wide[4:]),
-            "mc0": lambda: mix_c(0), "mc1": lambda: mix_c(1), "mc2": lambda: mix_c(2),
-            "qc0": lambda: quant_c(0), "qc1": lambda: quant_c(1), "qc2": lambda: quant_c(2),
-            "mb00": lambda: mix_b(0, 0), "mb01": lambda: mix_b(0, 1), "mb10": lambda: mix_b(1, 0), "mb11": lambda: mix_b(1, 1),
-            "qb0": lambda: quant_b(0), "qb1": lambda: quant_b(1),
-            "pt0": lambda: permute_words(t_code, t_raw, "t_code", 0), "pt1": lambda: permute_words(t_code, t_raw, "t_code", 1),
-            "pq0": lambda: permute_words(q_code, q_raw, "q_code", 0), "pq1": lambda: permute_words(q_code, q_raw, "q_code", 1),
-            "ps0": lambda: permute_scales(0), "ps1": lambda: permute_scales(1),
-            "mu": lambda: nc.vector.tensor_copy(out=mu_f32[:], in_=mu_raw[:]),
-            "f00": lambda: f_bank(0, 0, 0), "f01": lambda: f_bank(0, 1, 0), "e00": lambda: e_bank(0, 0, 0), "e01": lambda: e_bank(0, 1, 0),
-            "f10": lambda: run(f1[: len(f1) // 2]), "f11": lambda: run(f1[len(f1) // 2 :]),
-            "qh0": lambda: quant_h(0, 0), "qh1": lambda: quant_h(0, 1),
-        }
+        head = {"mt": mt_bank, "e": e_bank, "f": f_bank, "mb": mix_b, "qb": quant_b, "qh": quant_h, "mc": mix_c, "qc": quant_c,
+                "w": lambda k, g: run(steps(widen_b, k, two, four)[4 * g : 4 * g + 4]), "n": spread_norm, "m": m_bank,
+                "pt": lambda h: permute_words(t_code, t_raw, "t_code", h), "pq": lambda h: permute_words(q_code, q_raw, "q_code", h),
+                "d": warm_pe, "mS": lambda k, g: mix_b(k, g, nc.scalar.copy), "ps": permute_scales, "mu": lambda h: nc.vector.tensor_copy(out=mu_f32[:], in_=mu_raw[:])}
         for name in HEAD.split():
-            head[name]()
-        for k in range(chunks - 2):
+            n = 0
+            while not name[n] in "0123456789":
+                n += 1
+            head[name[:n]](*[int(ch) for ch in name[n:]])
+        for k in range(1, chunks - 2):
             run(steps(mt_bank, k, r_tiles, two))
             run(steps(widen_b, k + 2, two, four))
             run(steps(e_bank, k + 1, two, r_tiles))

@@ -19,38 +19,14 @@ ALU = mybir.AluOpType
 
 P = 128
 PACK = 4
+PASS = P * PACK
 BANK = 512
+BANKS = 8
+QUADS = 4
+T_ROW = 2 * PACK
 WIDTHS = (128, 256, 256, 256, 128)
-RUN = 4
-EARLY = 4
-TAIL = 2
-T1 = 1
-T2 = 2
-C_ON_S = (1,)
-LOADS = "id bs c0 b01 ts t0 q0 c1 qs mu t1 q1 p0 ps p1 c2 b2 c3"
-HEAD = "w00 w01 mc0 qc0 mb00 mb01 pt0 w10 w11 qb0 pq0 ps0 ps1 mu0 pt1 mc1 f000 f010 mb10 pq1 qc1 e000 mb11 e010 f100 f102 f110 f112 qb1 qh00 qh01 mc2 qc2 mt000 mt001 w20 w21 e100 e101 e110 e111 n0 f200 f202 f210 f212 qh10 qh11 mb20 mb21 m00 qb2 mc3 m04 qc3"
-LAG = {'wid': -250, 'mc': -224, 'qc': -200, 'mu': -278, 'w0': -94, 'w1': 10, 'mb': -160, 'qb': -130, 'f': 0, 'e': 100, 'qh': 150, 'mt': 350, 'n': 380, 'm': 640}
-B_LOADS = ([0], [1, 2], [3, 4])
-
-
-def weave(main, fillers):
-    done = 0
-    if len(main) == 0:
-        main = [lambda: None]
-    for n, step in enumerate(main):
-        step()
-        upto = min(len(fillers), -(-(n + 1) * len(fillers) // len(main)))
-        for filler in fillers[done:upto]:
-            filler()
-        done = upto
-
-
-def zipped(first, second):
-    steps = []
-    for n in range(max(len(first), len(second))):
-        steps.extend(first[n : n + 1])
-        steps.extend(second[n : n + 1])
-    return steps
+MIX_RUN = 4
+PAIR = 2
 
 
 def tile_cptensorsimultaneouspowerstep_w8_kernel(
@@ -58,302 +34,283 @@ def tile_cptensorsimultaneouspowerstep_w8_kernel(
 ):
     nc = tc.nc
     chunks = len(WIDTHS)
-    starts = [sum(WIDTHS[:k]) for k in range(chunks)]
+    last = chunks - 1
+    starts = [sum(WIDTHS[:k]) for k in range(chunks + 1)]
 
     with ExitStack() as ctx:
-        keep = ctx.enter_context(tc.tile_pool(name="keep", bufs=1))
-        stage = ctx.enter_context(tc.tile_pool(name="stage", bufs=3))
-        psum = ctx.enter_context(tc.psum_pool(name="psum", bufs=8))
+        sbuf = ctx.enter_context(tc.tile_pool(name="sbuf", bufs=1))
+        psum = ctx.enter_context(tc.psum_pool(name="psum", bufs=BANKS))
         ctx.enter_context(tc.manual_schedule())
 
         def kept(name, shape, dtype):
-            return keep.tile(shape, dtype, name=name, align_bytes=64)
+            return sbuf.tile(shape, dtype, name=name, align_bytes=64)
 
         def bank(name):
             return psum.tile([P, BANK], F32, name=name, tag="bank")
+
+        def mx(acc, stationary, moving, start, stop):
+            nc.tensor.matmul_mx(
+                out=acc, lhsT=stationary[0].bitcast(FP8X4), lhsT_scale=stationary[1],
+                rhs=moving[0].bitcast(FP8X4), rhs_scale=moving[1], start=start, stop=stop,
+            )
 
         qt_scale_raw = kept("qt_scale_raw", [P, S], U8)
         p_scale = kept("p_scale", [P, I], U8)
         nc.vector.memset(qt_scale_raw[:].bitcast(I32), 0)
         nc.vector.memset(p_scale[:].bitcast(I32), 0)
-        warm = kept("warm", [P, 8], F32)
-        nc.vector.memset(warm[:], 1.0)
-        nc.scalar.activation(out=warm[:, 4:5], in_=warm[:, 0:1], func=ACT.Abs_reciprocal_sqrt)
+        ident = kept("ident", [P, P], F32)
+        make_identity(nc, ident[:])
 
-        def load_scales(engine, tile, row0, scales):
-            groups = scales.shape[0]
-            for quad in range(4):
+        def load_scales(tile, row0, scales):
+            passes = scales.shape[0]
+            for quad in range(QUADS):
                 first = 32 * quad + row0
-                engine.dma_start(
-                    out=tile[first : first + 4 * groups, :].bitcast(I32),
-                    in_=scales[:, 4 * quad : 4 * quad + 4, :].bitcast(I32),
+                nc.sync.dma_start(
+                    out=tile[first : first + PACK * passes, :].bitcast(I32),
+                    in_=scales[:, PACK * quad : PACK * (quad + 1), :].bitcast(I32),
                 )
 
-        c_rows = c.rearrange("(p t) r -> p t r", t=PACK)
-        b_rows = b_bytes.rearrange("(g p t) r -> g p t r", p=P, t=PACK)
-        c_raw, b_raw = {}, {}
-
-        def load_c(ks):
-            r0, r1 = starts[ks[0]], starts[ks[-1]] + WIDTHS[ks[-1]]
-            tile = kept("c_raw%d" % ks[0], [P, PACK, r1 - r0], BF16)
-            nc.sync.dma_start(out=tile[:], in_=c_rows[:, :, r0:r1])
-            for k in ks:
-                c_raw[k] = tile[:, :, starts[k] - r0 : starts[k] - r0 + WIDTHS[k]]
-
-        def load_b(ks):
-            r0, r1 = starts[ks[0]], starts[ks[-1]] + WIDTHS[ks[-1]]
-            for g in range(2):
-                tile = kept("b_raw%d_%d" % (ks[0], g), [P, PACK, r1 - r0], U8)
-                nc.sync.dma_start(out=tile[:], in_=b_rows[g][:, :, r0:r1])
-                for k in ks:
-                    b_raw[k, g] = tile[:, :, starts[k] - r0 : starts[k] - r0 + WIDTHS[k]]
-
-        def load_words(name, words, n0, n1):
-            groups = words.shape[0]
-            tile = kept(name, [P, groups, n1 - n0], U32)
+        def load_words(name, words, half):
+            tile = kept("%s%d" % (name, half), [P, words.shape[0], PASS], U32)
+            columns = slice(PACK * PASS * half, PACK * PASS * (half + 1))
             nc.sync.dma_start(
                 out=tile[:].bitcast(I32),
-                in_=words.rearrange("g p n t -> p g (n t)")[:, :, PACK * n0 : PACK * n1].bitcast(I32),
+                in_=words.rearrange("g p n t -> p g (n t)")[:, :, columns].bitcast(I32),
             )
             return tile
 
+        def load_rows(name, rows, dtype, k0, k1):
+            tile = kept("%s_%d" % (name, k0), [P, PACK, starts[k1] - starts[k0]], dtype)
+            nc.sync.dma_start(out=tile[:], in_=rows[:, :, starts[k0] : starts[k1]])
+            return [tile[:, :, starts[k] - starts[k0] : starts[k + 1] - starts[k0]] for k in range(k0, k1)]
+
+        c_rows = c.rearrange("(p t) r -> p t r", t=PACK)
+        b_rows = b_bytes.rearrange("(g p t) r -> g p t r", p=P, t=PACK)
         b_scale_sb = kept("b_scale_sb", [P, 2, PACK], F32)
         mu_raw = kept("mu_raw", [P, 2, PACK], BF16)
-        t_raw, q_raw = {}, {}
 
-        ident = kept("ident", [P, P], F32)
-        p_code = {}
-        rest = list(range(2, chunks))
-        loads = {
-            "bs": lambda: nc.sync.dma_start(out=b_scale_sb[:], in_=b_scale.rearrange("(g p t) o -> p g (t o)", p=P, t=PACK)),
-            "mu": lambda: nc.sync.dma_start(out=mu_raw[:], in_=mu.rearrange("(g p t) -> p g t", p=P, t=PACK)),
-            "c0": lambda: load_c([0]), "c1": lambda: load_c([1]), "c01": lambda: load_c([0, 1]), "c2": lambda: load_c([2]), "c3": lambda: load_c(rest[1:]),
-            "b0": lambda: load_b([0]), "b1": lambda: load_b([1]), "b01": lambda: load_b([0, 1]), "b2": lambda: load_b(rest),
-            "t0": lambda: t_raw.setdefault(0, load_words("t_raw0", t_words, 0, 512)),
-            "t1": lambda: t_raw.setdefault(1, load_words("t_raw1", t_words, 512, 1024)),
-            "q0": lambda: q_raw.setdefault(0, load_words("q_raw0", q_words, 0, 512)),
-            "q1": lambda: q_raw.setdefault(1, load_words("q_raw1", q_words, 512, 1024)),
-            "p0": lambda: p_code.setdefault(0, load_words("p_code0", p_words, 0, 512)),
-            "p1": lambda: p_code.setdefault(1, load_words("p_code1", p_words, 512, 1024)),
-            "qs": lambda: load_scales(nc.sync, qt_scale_raw, 0, q_scales),
-            "ts": lambda: load_scales(nc.sync, qt_scale_raw, 8, t_scales),
-            "tsG": lambda: load_scales(nc.gpsimd, qt_scale_raw, 8, t_scales),
-            "psG": lambda: load_scales(nc.gpsimd, p_scale, 0, p_scales),
-            "muG": lambda: nc.gpsimd.dma_start(out=mu_raw[:], in_=mu.rearrange("(g p t) -> p g t", p=P, t=PACK)),
-            "id": lambda: make_identity(nc, ident[:]),
-            "ps": lambda: load_scales(nc.sync, p_scale, 0, p_scales),
-        }
-        for name in LOADS.split():
-            loads[name]()
+        nc.sync.dma_start(out=b_scale_sb[:], in_=b_scale.rearrange("(g p t) o -> p g (t o)", p=P, t=PACK))
+        c_raw = load_rows("c_raw", c_rows, BF16, 0, 1)
+        b_raw = [load_rows("b_raw%d" % g, b_rows[g], U8, 0, 2) for g in range(2)]
+        load_scales(qt_scale_raw, T_ROW, t_scales)
+        t_raw = [load_words("t_raw", t_words, 0)]
+        q_raw = [load_words("q_raw", q_words, 0)]
+        c_raw.extend(load_rows("c_raw", c_rows, BF16, 1, 2))
+        load_scales(qt_scale_raw, 0, q_scales)
+        nc.sync.dma_start(out=mu_raw[:], in_=mu.rearrange("(g p t) -> p g t", p=P, t=PACK))
+        t_raw.append(load_words("t_raw", t_words, 1))
+        q_raw.append(load_words("q_raw", q_words, 1))
+        p_code = [load_words("p_code", p_words, 0)]
+        load_scales(p_scale, 0, p_scales)
+        p_code.append(load_words("p_code", p_words, 1))
+        c_raw.extend(load_rows("c_raw", c_rows, BF16, 2, 3))
+        for g in range(2):
+            b_raw[g].extend(load_rows("b_raw%d" % g, b_rows[g], U8, 2, chunks))
+        c_raw.extend(load_rows("c_raw", c_rows, BF16, 3, chunks))
 
-        mu_f32 = kept("mu_f32", [P, 2, PACK], F32)
-        t_code, q_code, qt_scale = {}, {}, {}
-
-        def permute_words(dst, src, name, half):
-            groups = src[half].shape[1]
-            dst[half] = kept("%s%d" % (name, half), [P, groups, PACK, P], U32)
+        def permute_words(name, raw):
+            tile = kept(name, [P, raw.shape[1], PACK, P], U32)
             nc.vector.tensor_copy(
-                out=dst[half][:].bitcast(I32).rearrange("p g t (c i) -> p g c t i", i=PACK),
-                in_=src[half][:].bitcast(I32).rearrange("p g (c i t) -> p g c t i", i=PACK, t=PACK),
+                out=tile[:].bitcast(I32).rearrange("p g t (a i) -> p g a t i", i=PACK),
+                in_=raw[:].bitcast(I32).rearrange("p g (a i t) -> p g a t i", i=PACK, t=PACK),
             )
+            return tile
 
         def permute_scales(half):
-            qt_scale[half] = kept("qt_scale%d" % half, [P, PACK, P], U8)
+            tile = kept("qt_scale%d" % half, [P, PACK, P], U8)
             nc.vector.tensor_copy(
-                out=qt_scale[half][:],
-                in_=qt_scale_raw[:, 512 * half : 512 * (half + 1)].rearrange("p (m t) -> p t m", t=PACK),
+                out=tile[:],
+                in_=qt_scale_raw[:, PASS * half : PASS * (half + 1)].rearrange("p (m t) -> p t m", t=PACK),
             )
+            return tile
 
-        b_wide, b_mixed, c_mixed, f_sb, h_mixed = {}, {}, {}, {}, {}
-        b_code, b_sc, c_code, c_sc, h_code, h_sc = {}, {}, {}, {}, {}, {}
-        ssq, rnorm = {}, {}
+        t_code, q_code, qt_scale = {}, {}, {}
+        mu_f32 = kept("mu_f32", [P, 2, PACK], F32)
 
-        def widen_b(k, g, t):
-            if t == 0:
-                b_wide[k, g] = stage.tile([P, PACK, WIDTHS[k]], BF16, name="b_wide%d_%d" % (k, g), tag="b_wide", bufs=6)
-            nc.scalar.activation(
-                out=b_wide[k, g][:, t, :], in_=b_raw[k, g][:, t, :].bitcast(FP8), func=ACT.Copy,
-                scale=b_scale_sb[:, g, t : t + 1],
-            )
+        b_wide, b_mixed, c_mixed, h_mixed, mu_f = {}, {}, {}, {}, {}
+        b_mx, c_mx, h_mx, ssq, factor = {}, {}, {}, {}, {}
 
-        def interleave(dst, src, copy=nc.vector.tensor_copy):
+        def widen_b(k):
+            for g in range(2):
+                b_wide[k, g] = kept("b_wide%d_%d" % (k, g), [P, PACK, WIDTHS[k]], BF16)
+                for t in range(PACK):
+                    nc.scalar.activation(
+                        out=b_wide[k, g][:, t, :], in_=b_raw[g][k][:, t, :].bitcast(FP8), func=ACT.Copy,
+                        scale=b_scale_sb[:, g, t : t + 1],
+                    )
+
+        def interleave(copy, mixed, rows):
             copy(
-                out=dst.rearrange("p (c i) t -> p c t i", i=RUN),
-                in_=src.rearrange("p t (c i) -> p c t i", i=RUN),
+                out=mixed.rearrange("p (a i) t -> p a t i", i=MIX_RUN),
+                in_=rows.rearrange("p t (a i) -> p a t i", i=MIX_RUN),
             )
 
-        def mix_b(k, g, copy=nc.vector.tensor_copy):
-            if k not in b_mixed:
-                b_mixed[k] = stage.tile([P, 2, WIDTHS[k], PACK], BF16, name="b_mixed%d" % k, tag="b_mixed", align_bytes=64, bufs=3)
-            interleave(b_mixed[k][:, g], b_wide[k, g][:], copy)
+        def quantize(name, mixed, width):
+            words = kept(name + "_words", [P, width], U32)
+            scales = kept(name + "_scales", [P, width], U8)
+            nc.vector.quantize_mx(out=words[:].bitcast(FP8X4), scales=scales[:], in_=mixed)
+            return words, scales
 
-        def mix_c(k):
-            c_mixed[k] = stage.tile([P, WIDTHS[k], PACK], BF16, name="c_mixed%d" % k, tag="c_mixed", align_bytes=64, bufs=3)
-            interleave(c_mixed[k][:], c_raw[k], nc.scalar.copy if k in C_ON_S else nc.vector.tensor_copy)
-
-        def quantize(name, codes, scales, key, width, src):
-            codes[key] = kept(name + "_code", [P, width], U32)
-            scales[key] = kept(name + "_sc", [P, width], U8)
-            nc.vector.quantize_mx(out=codes[key][:].bitcast(FP8X4), scales=scales[key][:], in_=src)
+        def mix_b(k, g):
+            if g == 0:
+                b_mixed[k] = kept("b_mixed%d" % k, [P, 2, WIDTHS[k], PACK], BF16)
+            interleave(nc.vector.tensor_copy, b_mixed[k][:, g], b_wide[k, g][:])
 
         def quant_b(k):
-            quantize("b%d" % k, b_code, b_sc, k, 2 * WIDTHS[k], b_mixed[k][:].rearrange("p g r t -> p (g r t)"))
+            b_mx[k] = quantize("b%d" % k, b_mixed[k][:].rearrange("p g r t -> p (g r t)"), 2 * WIDTHS[k])
+
+        def mix_c(k, copy=nc.vector.tensor_copy):
+            c_mixed[k] = kept("c_mixed%d" % k, [P, WIDTHS[k], PACK], BF16)
+            interleave(copy, c_mixed[k][:], c_raw[k])
 
         def quant_c(k):
-            quantize("c%d" % k, c_code, c_sc, k, WIDTHS[k], c_mixed[k][:].rearrange("p r t -> p (r t)"))
+            c_mx[k] = quantize("c%d" % k, c_mixed[k][:].rearrange("p r t -> p (r t)"), WIDTHS[k])
 
-        def quant_h(k, half):
-            quantize("h%d_%d" % (k, half), h_code, h_sc, (k, half), WIDTHS[k],
-                     h_mixed[k, half][:].rearrange("p r t -> p (r t)"))
-
-        def f_bank(k, half, t0):
+        def make_f(k):
             w = WIDTHS[k]
-            if (k, half) not in f_sb:
-                f_sb[k, half] = stage.tile([P, PACK, w], F32, name="f_sb%d_%d" % (k, half), tag="f_sb", bufs=6)
-            acc = bank("f_acc%d_%d_%d" % (k, half, t0))
-            slots = range(t0, t0 + BANK // w)
-            for t in slots:
-                nc.tensor.matmul_mx(
-                    out=acc[:, (t - t0) * w : (t - t0 + 1) * w],
-                    lhsT=t_code[half][:, 0, t, :].bitcast(FP8X4), lhsT_scale=qt_scale[half][8:P, t, :],
-                    rhs=c_code[k][:].bitcast(FP8X4), rhs_scale=c_sc[k][:], start=True, stop=True,
-                )
-            for t in slots:
-                nc.scalar.activation(
-                    out=f_sb[k, half][:, t, :], in_=acc[:, (t - t0) * w : (t - t0 + 1) * w], func=ACT.Copy,
-                    scale=mu_f32[:, half, t : t + 1],
-                )
-
-        def e_bank(k, half, rt):
-            w = WIDTHS[k]
-            if (k, half) not in h_mixed:
-                h_mixed[k, half] = stage.tile([P, w, PACK], BF16, name="h_mixed%d_%d" % (k, half), tag="h_mixed", align_bytes=64, bufs=6)
-            acc = bank("e_acc%d_%d_%d" % (k, half, rt))
-            for t in range(PACK):
-                for g in range(2):
-                    cols = slice(g * w + rt * P, g * w + (rt + 1) * P)
-                    nc.tensor.matmul_mx(
-                        out=acc[:, t * P : (t + 1) * P],
-                        lhsT=q_code[half][:, g, t, :].bitcast(FP8X4), lhsT_scale=qt_scale[half][4 * g : P, t, :],
-                        rhs=b_code[k][:, cols].bitcast(FP8X4), rhs_scale=b_sc[k][:, cols],
-                        start=(g == 0), stop=(g == 1),
-                    )
-            cols = slice(rt * P, (rt + 1) * P)
-            nc.vector.tensor_tensor(
-                out=h_mixed[k, half][:, cols, :].rearrange("p (c i) t -> p c t i", i=2),
-                in0=acc[:].rearrange("p (t c i) -> p c t i", t=PACK, i=2),
-                in1=f_sb[k, half][:, :, cols].rearrange("p t (c i) -> p c t i", i=2),
-                op=ALU.mult,
-            )
-
-        def mt_bank(k, rt, ih):
-            if k not in ssq:
-                ssq[k] = kept("ssq%d" % k, [P, 2 * WIDTHS[k] // P], F32)
-            acc = bank("mt_acc%d_%d_%d" % (k, rt, ih))
-            cols, rows = slice(rt * P, (rt + 1) * P), slice(ih * BANK, (ih + 1) * BANK)
+            per_bank = BANK // w
             for half in range(2):
-                nc.tensor.matmul_mx(
-                    out=acc[:],
-                    lhsT=h_code[k, half][:, cols].bitcast(FP8X4), lhsT_scale=h_sc[k, half][:, cols],
-                    rhs=p_code[ih][:, half, :].bitcast(FP8X4), rhs_scale=p_scale[4 * half : P, rows],
-                    start=(half == 0), stop=(half == 1),
-                )
-            squares = stage.tile([P, BANK], F32, name="squares%d_%d_%d" % (k, rt, ih), tag="squares")
-            nc.scalar.activation(out=squares[:], in_=acc[:], func=ACT.Square,
-                                 accum_out=ssq[k][:, 2 * rt + ih : 2 * rt + ih + 1])
+                mu_f[k, half] = kept("mu_f%d_%d" % (k, half), [P, PACK, w], F32)
+                for t0 in range(0, PACK, per_bank):
+                    acc = bank("f_acc%d_%d_%d" % (k, half, t0))
+                    for n in range(per_bank):
+                        weights = (t_code[half][:, 0, t0 + n, :], qt_scale[half][T_ROW:P, t0 + n, :])
+                        mx(acc[:, n * w : (n + 1) * w], weights, (c_mx[k][0][:], c_mx[k][1][:]), True, True)
+                    for n in range(per_bank):
+                        nc.scalar.activation(
+                            out=mu_f[k, half][:, t0 + n, :], in_=acc[:, n * w : (n + 1) * w], func=ACT.Copy,
+                            scale=mu_f32[:, half, t0 + n : t0 + n + 1],
+                        )
 
-        def spread_norm(k):
+        def make_h(k, half):
+            w = WIDTHS[k]
+            h_mixed[k, half] = kept("h_mixed%d_%d" % (k, half), [P, w, PACK], BF16)
+            for r0 in range(0, w, P):
+                acc = bank("e_acc%d_%d_%d" % (k, half, r0))
+                for t in range(PACK):
+                    for g in range(2):
+                        cols = slice(g * w + r0, g * w + r0 + P)
+                        weights = (q_code[half][:, g, t, :], qt_scale[half][PACK * g : P, t, :])
+                        mx(acc[:, t * P : (t + 1) * P], weights, (b_mx[k][0][:, cols], b_mx[k][1][:, cols]),
+                           g == 0, g == 1)
+                nc.vector.tensor_tensor(
+                    out=h_mixed[k, half][:, r0 : r0 + P, :].rearrange("p (a i) t -> p a t i", i=PAIR),
+                    in0=acc[:].rearrange("p (t a i) -> p a t i", t=PACK, i=PAIR),
+                    in1=mu_f[k, half][:, :, r0 : r0 + P].rearrange("p t (a i) -> p a t i", i=PAIR),
+                    op=ALU.mult,
+                )
+
+        def quant_h(k):
+            for half in range(2):
+                mixed = h_mixed[k, half][:].rearrange("p r t -> p (r t)")
+                h_mx[k, half] = quantize("h%d_%d" % (k, half), mixed, WIDTHS[k])
+
+        def sum_squares(k):
+            ssq[k] = kept("ssq%d" % k, [P, 2 * WIDTHS[k] // P], F32)
+            for n in range(WIDTHS[k] // P):
+                cols = slice(n * P, (n + 1) * P)
+                for part in range(2):
+                    acc = bank("mt_acc%d_%d_%d" % (k, n, part))
+                    rows = slice(part * BANK, (part + 1) * BANK)
+                    for half in range(2):
+                        mx(acc[:], (h_mx[k, half][0][:, cols], h_mx[k, half][1][:, cols]),
+                           (p_code[part][:, half, :], p_scale[PACK * half : P, rows]), half == 0, half == 1)
+                    squares = sbuf.tile([P, BANK], F32, name="squares%d_%d_%d" % (k, n, part), tag="squares", bufs=3)
+                    nc.scalar.activation(
+                        out=squares[:], in_=acc[:], func=ACT.Square,
+                        accum_out=ssq[k][:, 2 * n + part : 2 * n + part + 1],
+                    )
+
+        def make_factor(k):
             w = WIDTHS[k]
             acc = bank("ssq_acc%d" % k)
-            for rt in range(w // P):
-                for ih in range(2):
-                    col = 2 * rt + ih
+            for n in range(w // P):
+                for part in range(2):
                     nc.tensor.matmul(
-                        out=acc[:, rt * P : (rt + 1) * P],
-                        lhsT=ssq[k][:, col : col + 1].to_broadcast([P, P]), rhs=ident[:],
-                        start=(ih == 0), stop=(ih == 1), is_transpose=True,
+                        out=acc[:, n * P : (n + 1) * P],
+                        lhsT=ssq[k][:, 2 * n + part : 2 * n + part + 1].to_broadcast([P, P]), rhs=ident[:],
+                        start=(part == 0), stop=(part == 1), is_transpose=True,
                     )
-            rnorm[k] = kept("rnorm%d" % k, [P, w], F32)
-            nc.scalar.activation(out=rnorm[k][:], in_=acc[:, 0:w], func=ACT.Abs_reciprocal_sqrt,
-                                 scale=1.0 / I, bias=EPS)
+            factor[k] = kept("factor%d" % k, [P, w], F32)
+            nc.scalar.activation(
+                out=factor[k][:], in_=acc[:, 0:w], func=ACT.Abs_reciprocal_sqrt, scale=1.0 / I, bias=EPS
+            )
 
         out_rows = out.rearrange("(a p) r -> p a r", p=P)
 
-        def m_bank(k, a0):
+        def make_out(k, a0):
             w = WIDTHS[k]
             tiles = BANK // w
             acc = bank("m_acc%d_%d" % (k, a0))
-            for a in range(a0, a0 + tiles):
-                rows = slice(a * P, (a + 1) * P)
+            for n in range(tiles):
+                part, row0 = divmod((a0 + n) * P, PASS)
+                rows = slice((a0 + n) * P, (a0 + n + 1) * P)
                 for half in range(2):
-                    nc.tensor.matmul_mx(
-                        out=acc[:, (a - a0) * w : (a - a0 + 1) * w],
-                        lhsT=p_code[a // 4][:, half, (a % 4) * P : (a % 4 + 1) * P].bitcast(FP8X4), lhsT_scale=p_scale[4 * half : P, rows],
-                        rhs=h_code[k, half][:].bitcast(FP8X4), rhs_scale=h_sc[k, half][:],
-                        start=(half == 0), stop=(half == 1),
-                    )
-            result = stage.tile([P, tiles, w], F32, name="result%d_%d" % (k, a0), tag="result", bufs=8)
+                    mx(acc[:, n * w : (n + 1) * w],
+                       (p_code[part][:, half, row0 : row0 + P], p_scale[PACK * half : P, rows]),
+                       (h_mx[k, half][0][:], h_mx[k, half][1][:]), half == 0, half == 1)
+            result = kept("result%d_%d" % (k, a0), [P, tiles, w], F32)
             nc.vector.tensor_tensor(
                 out=result[:], in0=acc[:].rearrange("p (a r) -> p a r", a=tiles),
-                in1=rnorm[k][:].unsqueeze(1).to_broadcast([P, tiles, w]), op=ALU.mult,
+                in1=factor[k][:].unsqueeze(1).to_broadcast([P, tiles, w]), op=ALU.mult,
             )
-            nc.sync.dma_start(out=out_rows[:, a0 : a0 + tiles, starts[k] : starts[k] + w], in_=result[:])
+            nc.sync.dma_start(out=out_rows[:, a0 : a0 + tiles, starts[k] : starts[k + 1]], in_=result[:])
 
-        def warm_pe(count):
-            acc = bank("warm_acc")
-            src = c_mixed[0][:].rearrange("p r t -> p (r t)")
-            for n in range(count):
-                nc.tensor.matmul(out=acc[:], lhsT=src[:, 0:P], rhs=src, start=True, stop=True)
+        widen_b(0)
+        widen_b(1)
+        mix_c(0)
+        quant_c(0)
+        mix_b(0, 0)
+        mix_b(0, 1)
+        t_code[0] = permute_words("t_code0", t_raw[0])
+        quant_b(0)
+        q_code[0] = permute_words("q_code0", q_raw[0])
+        qt_scale[0] = permute_scales(0)
+        qt_scale[1] = permute_scales(1)
+        nc.vector.tensor_copy(out=mu_f32[:], in_=mu_raw[:])
+        t_code[1] = permute_words("t_code1", t_raw[1])
+        mix_c(1, nc.scalar.copy)
+        make_f(0)
+        mix_b(1, 0)
+        q_code[1] = permute_words("q_code1", q_raw[1])
+        quant_c(1)
+        make_h(0, 0)
+        mix_b(1, 1)
+        quant_b(1)
+        make_h(0, 1)
+        make_f(1)
+        quant_h(0)
+        make_h(1, 0)
+        sum_squares(0)
+        mix_c(2)
+        quant_c(2)
 
-        def steps(fn, k, *ranges):
-            if k < 0 or k >= chunks:
-                return []
-            w = WIDTHS[k]
-            args = [()]
-            for rng in ranges:
-                args = [a + (x,) for a in args for x in rng(w)]
-            return [(lambda a=a: fn(k, *a)) for a in args]
-
-        two = lambda w: range(2)
-        four = lambda w: range(PACK)
-        r_tiles = lambda w: range(w // P)
-        t_starts = lambda w: range(0, PACK, BANK // w)
-        a_starts = lambda w: range(0, I // P, BANK // w)
-
-        def run(todo):
-            for step in todo:
-                step()
-
-        head = {"mt": mt_bank, "e": e_bank, "f": f_bank, "mb": mix_b, "qb": quant_b, "qh": quant_h, "mc": mix_c, "qc": quant_c,
-                "w": lambda k, g: run(steps(widen_b, k, two, four)[4 * g : 4 * g + 4]), "n": spread_norm, "m": m_bank,
-                "pt": lambda h: permute_words(t_code, t_raw, "t_code", h), "pq": lambda h: permute_words(q_code, q_raw, "q_code", h),
-                "d": warm_pe, "mS": lambda k, g: mix_b(k, g, nc.scalar.copy), "ps": permute_scales, "mu": lambda h: nc.vector.tensor_copy(out=mu_f32[:], in_=mu_raw[:])}
-        for name in HEAD.split():
-            n = 0
-            while not name[n] in "0123456789":
-                n += 1
-            head[name[:n]](*[int(ch) for ch in name[n:]])
-        for k in range(1, chunks - 2):
-            run(steps(mt_bank, k, r_tiles, two))
-            run(steps(widen_b, k + 2, two, four))
-            run(steps(e_bank, k + 1, two, r_tiles))
-            run(steps(spread_norm, k))
-            run(steps(f_bank, k + 2, two, t_starts))
-            run(steps(quant_h, k + 1, two))
-            run(steps(mix_b, k + 2, two))
-            weave(steps(m_bank, k, a_starts), steps(quant_b, k + 2) + steps(mix_c, k + 3) + steps(quant_c, k + 3))
-        k = chunks - 2
-        mt = steps(mt_bank, k, r_tiles, two)
-        m = steps(m_bank, k, a_starts)
-        run(mt[:T1])
-        run(steps(e_bank, k + 1, two, r_tiles))
-        run(mt[T1:])
-        run(steps(quant_h, k + 1, two))
-        mt = steps(mt_bank, k + 1, r_tiles, two)
-        run(mt[:T2])
-        run(steps(spread_norm, k))
-        run(mt[T2:])
-        run(m[:TAIL])
-        run(steps(spread_norm, k + 1))
-        run(m[TAIL:])
-        run(steps(m_bank, k + 1, a_starts))
+        for k in range(chunks):
+            if k + 2 <= last:
+                widen_b(k + 2)
+            if k + 1 <= last:
+                for half in range(1 if k == 0 else 0, 2):
+                    make_h(k + 1, half)
+            make_factor(k)
+            if k + 2 <= last:
+                make_f(k + 2)
+            if k + 1 <= last:
+                quant_h(k + 1)
+            between = []
+            if k + 2 <= last:
+                mix_b(k + 2, 0)
+                mix_b(k + 2, 1)
+                between.append((quant_b, k + 2))
+            if k + 3 <= last:
+                between.extend([(mix_c, k + 3), (quant_c, k + 3)])
+            firsts = list(range(0, I // P, BANK // WIDTHS[k]))
+            sums_after = len(firsts) // 2 if k + 1 == last else len(firsts)
+            done = 0
+            for n, a0 in enumerate(firsts):
+                make_out(k, a0)
+                upto = ((n + 1) * len(between) + len(firsts) - 1) // len(firsts)
+                for step, chunk in between[done:upto]:
+                    step(chunk)
+                done = upto
+                if n + 1 == sums_after and k + 1 <= last:
+                    sum_squares(k + 1)

@@ -58,6 +58,9 @@ def tile_cptensorsimultaneouspowerstep_w8_kernel(
         p_scale = kept("p_scale", [P, I], U8)
         nc.vector.memset(qt_scale_raw[:].bitcast(I32), 0)
         nc.vector.memset(p_scale[:].bitcast(I32), 0)
+        table_warmup = kept("table_warmup", [P, 8], F32)
+        nc.vector.memset(table_warmup[:], 1.0)
+        nc.scalar.activation(out=table_warmup[:, 4:5], in_=table_warmup[:, 0:1], func=ACT.Abs_reciprocal_sqrt)
         ident = kept("ident", [P, P], F32)
         make_identity(nc, ident[:])
 

from contextlib import ExitStack

import concourse.mybir as mybir
from concourse.masks import make_identity

I, J, K, S, R = 1024, 1024, 512, 1024, 1024
EPS = 1e-6
FLOPS = 2 * S * R * (J + K + I)

F32 = mybir.dt.float32
BF16 = mybir.dt.bfloat16
U32 = mybir.dt.uint32
I32 = mybir.dt.int32
U8 = mybir.dt.uint8
FP8 = mybir.dt.float8_e4m3fn
FP8X4 = mybir.dt.float8_e4m3fn_x4
ACT = mybir.ActivationFunctionType
ALU = mybir.AluOpType

P = 128
PACK = 4
PASS = P * PACK
BANK = 512
BANKS = 8
QUADS = 4
T_ROW = 2 * PACK
WIDTHS = (128, 256, 256, 256, 128)
MIX_RUN = 4
PAIR = 2


def tile_cptensorsimultaneouspowerstep_w8_kernel(
    tc, p_words, p_scales, q_words, q_scales, t_words, t_scales, mu, b_bytes, b_scale, c, out
):
    nc = tc.nc
    chunks = len(WIDTHS)
    last = chunks - 1
    starts = [sum(WIDTHS[:k]) for k in range(chunks + 1)]

    with ExitStack() as ctx:
        sbuf = ctx.enter_context(tc.tile_pool(name="sbuf", bufs=1))
        psum = ctx.enter_context(tc.psum_pool(name="psum", bufs=BANKS))
        ctx.enter_context(tc.manual_schedule())

        def kept(name, shape, dtype):
            return sbuf.tile(shape, dtype, name=name, align_bytes=64)

        def bank(name):
            return psum.tile([P, BANK], F32, name=name, tag="bank")

        def mx(acc, stationary, moving, start, stop):
            nc.tensor.matmul_mx(
                out=acc, lhsT=stationary[0].bitcast(FP8X4), lhsT_scale=stationary[1],
                rhs=moving[0].bitcast(FP8X4), rhs_scale=moving[1], start=start, stop=stop,
            )

        qt_scale_raw = kept("qt_scale_raw", [P, S], U8)
        p_scale = kept("p_scale", [P, I], U8)
        nc.vector.memset(qt_scale_raw[:].bitcast(I32), 0)
        nc.vector.memset(p_scale[:].bitcast(I32), 0)
        table_warmup = kept("table_warmup", [P, 8], F32)
        nc.vector.memset(table_warmup[:], 1.0)
        nc.scalar.activation(out=table_warmup[:, 4:5], in_=table_warmup[:, 0:1], func=ACT.Abs_reciprocal_sqrt)
        ident = kept("ident", [P, P], F32)
        make_identity(nc, ident[:])

        def load_scales(tile, row0, scales):
            passes = scales.shape[0]
            for quad in range(QUADS):
                first = 32 * quad + row0
                nc.sync.dma_start(
                    out=tile[first : first + PACK * passes, :].bitcast(I32),
                    in_=scales[:, PACK * quad : PACK * (quad + 1), :].bitcast(I32),
                )

        def load_words(name, words, half):
            tile = kept("%s%d" % (name, half), [P, words.shape[0], PASS], U32)
            columns = slice(PACK * PASS * half, PACK * PASS * (half + 1))
            nc.sync.dma_start(
                out=tile[:].bitcast(I32),
                in_=words.rearrange("g p n t -> p g (n t)")[:, :, columns].bitcast(I32),
            )
            return tile

        def load_rows(name, rows, dtype, k0, k1):
            tile = kept("%s_%d" % (name, k0), [P, PACK, starts[k1] - starts[k0]], dtype)
            nc.sync.dma_start(out=tile[:], in_=rows[:, :, starts[k0] : starts[k1]])
            return [tile[:, :, starts[k] - starts[k0] : starts[k + 1] - starts[k0]] for k in range(k0, k1)]

        c_rows = c.rearrange("(p t) r -> p t r", t=PACK)
        b_rows = b_bytes.rearrange("(g p t) r -> g p t r", p=P, t=PACK)
        b_scale_sb = kept("b_scale_sb", [P, 2, PACK], F32)
        mu_raw = kept("mu_raw", [P, 2, PACK], BF16)

        nc.sync.dma_start(out=b_scale_sb[:], in_=b_scale.rearrange("(g p t) o -> p g (t o)", p=P, t=PACK))
        c_raw = load_rows("c_raw", c_rows, BF16, 0, 1)
        b_raw = [load_rows("b_raw%d" % g, b_rows[g], U8, 0, 2) for g in range(2)]
        load_scales(qt_scale_raw, T_ROW, t_scales)
        t_raw = [load_words("t_raw", t_words, 0)]
        q_raw = [load_words("q_raw", q_words, 0)]
        c_raw.extend(load_rows("c_raw", c_rows, BF16, 1, 2))
        load_scales(qt_scale_raw, 0, q_scales)
        nc.sync.dma_start(out=mu_raw[:], in_=mu.rearrange("(g p t) -> p g t", p=P, t=PACK))
        t_raw.append(load_words("t_raw", t_words, 1))
        q_raw.append(load_words("q_raw", q_words, 1))
        p_code = [load_words("p_code", p_words, 0)]
        load_scales(p_scale, 0, p_scales)
        p_code.append(load_words("p_code", p_words, 1))
        c_raw.extend(load_rows("c_raw", c_rows, BF16, 2, 3))
        for g in range(2):
            b_raw[g].extend(load_rows("b_raw%d" % g, b_rows[g], U8, 2, chunks))
        c_raw.extend(load_rows("c_raw", c_rows, BF16, 3, chunks))

        def permute_words(name, raw):
            tile = kept(name, [P, raw.shape[1], PACK, P], U32)
            nc.vector.tensor_copy(
                out=tile[:].bitcast(I32).rearrange("p g t (a i) -> p g a t i", i=PACK),
                in_=raw[:].bitcast(I32).rearrange("p g (a i t) -> p g a t i", i=PACK, t=PACK),
            )
            return tile

        def permute_scales(half):
            tile = kept("qt_scale%d" % half, [P, PACK, P], U8)
            nc.vector.tensor_copy(
                out=tile[:],
                in_=qt_scale_raw[:, PASS * half : PASS * (half + 1)].rearrange("p (m t) -> p t m", t=PACK),
            )
            return tile

        t_code, q_code, qt_scale = {}, {}, {}
        mu_f32 = kept("mu_f32", [P, 2, PACK], F32)

        b_wide, b_mixed, c_mixed, h_mixed, mu_f = {}, {}, {}, {}, {}
        b_mx, c_mx, h_mx, ssq, factor = {}, {}, {}, {}, {}

        def widen_b(k):
            for g in range(2):
                b_wide[k, g] = kept("b_wide%d_%d" % (k, g), [P, PACK, WIDTHS[k]], BF16)
                for t in range(PACK):
                    nc.scalar.activation(
                        out=b_wide[k, g][:, t, :], in_=b_raw[g][k][:, t, :].bitcast(FP8), func=ACT.Copy,
                        scale=b_scale_sb[:, g, t : t + 1],
                    )

        def interleave(copy, mixed, rows):
            copy(
                out=mixed.rearrange("p (a i) t -> p a t i", i=MIX_RUN),
                in_=rows.rearrange("p t (a i) -> p a t i", i=MIX_RUN),
            )

        def quantize(name, mixed, width):
            words = kept(name + "_words", [P, width], U32)
            scales = kept(name + "_scales", [P, width], U8)
            nc.vector.quantize_mx(out=words[:].bitcast(FP8X4), scales=scales[:], in_=mixed)
            return words, scales

        def mix_b(k, g):
            if g == 0:
                b_mixed[k] = kept("b_mixed%d" % k, [P, 2, WIDTHS[k], PACK], BF16)
            interleave(nc.vector.tensor_copy, b_mixed[k][:, g], b_wide[k, g][:])

        def quant_b(k):
            b_mx[k] = quantize("b%d" % k, b_mixed[k][:].rearrange("p g r t -> p (g r t)"), 2 * WIDTHS[k])

        def mix_c(k, copy=nc.vector.tensor_copy):
            c_mixed[k] = kept("c_mixed%d" % k, [P, WIDTHS[k], PACK], BF16)
            interleave(copy, c_mixed[k][:], c_raw[k])

        def quant_c(k):
            c_mx[k] = quantize("c%d" % k, c_mixed[k][:].rearrange("p r t -> p (r t)"), WIDTHS[k])

        def make_f(k):
            w = WIDTHS[k]
            per_bank = BANK // w
            for half in range(2):
                mu_f[k, half] = kept("mu_f%d_%d" % (k, half), [P, PACK, w], F32)
                for t0 in range(0, PACK, per_bank):
                    acc = bank("f_acc%d_%d_%d" % (k, half, t0))
                    for n in range(per_bank):
                        weights = (t_code[half][:, 0, t0 + n, :], qt_scale[half][T_ROW:P, t0 + n, :])
                        mx(acc[:, n * w : (n + 1) * w], weights, (c_mx[k][0][:], c_mx[k][1][:]), True, True)
                    for n in range(per_bank):
                        nc.scalar.activation(
                            out=mu_f[k, half][:, t0 + n, :], in_=acc[:, n * w : (n + 1) * w], func=ACT.Copy,
                            scale=mu_f32[:, half, t0 + n : t0 + n + 1],
                        )

        def make_h(k, half):
            w = WIDTHS[k]
            h_mixed[k, half] = kept("h_mixed%d_%d" % (k, half), [P, w, PACK], BF16)
            for r0 in range(0, w, P):
                acc = bank("e_acc%d_%d_%d" % (k, half, r0))
                for t in range(PACK):
                    for g in range(2):
                        cols = slice(g * w + r0, g * w + r0 + P)
                        weights = (q_code[half][:, g, t, :], qt_scale[half][PACK * g : P, t, :])
                        mx(acc[:, t * P : (t + 1) * P], weights, (b_mx[k][0][:, cols], b_mx[k][1][:, cols]),
                           g == 0, g == 1)
                nc.vector.tensor_tensor(
                    out=h_mixed[k, half][:, r0 : r0 + P, :].rearrange("p (a i) t -> p a t i", i=PAIR),
                    in0=acc[:].rearrange("p (t a i) -> p a t i", t=PACK, i=PAIR),
                    in1=mu_f[k, half][:, :, r0 : r0 + P].rearrange("p t (a i) -> p a t i", i=PAIR),
                    op=ALU.mult,
                )

        def quant_h(k):
            for half in range(2):
                mixed = h_mixed[k, half][:].rearrange("p r t -> p (r t)")
                h_mx[k, half] = quantize("h%d_%d" % (k, half), mixed, WIDTHS[k])

        def sum_squares(k):
            ssq[k] = kept("ssq%d" % k, [P, 2 * WIDTHS[k] // P], F32)
            for n in range(WIDTHS[k] // P):
                cols = slice(n * P, (n + 1) * P)
                for part in range(2):
                    acc = bank("mt_acc%d_%d_%d" % (k, n, part))
                    rows = slice(part * BANK, (part + 1) * BANK)
                    for half in range(2):
                        mx(acc[:], (h_mx[k, half][0][:, cols], h_mx[k, half][1][:, cols]),
                           (p_code[part][:, half, :], p_scale[PACK * half : P, rows]), half == 0, half == 1)
                    squares = sbuf.tile([P, BANK], F32, name="squares%d_%d_%d" % (k, n, part), tag="squares", bufs=3)
                    nc.scalar.activation(
                        out=squares[:], in_=acc[:], func=ACT.Square,
                        accum_out=ssq[k][:, 2 * n + part : 2 * n + part + 1],
                    )

        def make_factor(k):
            w = WIDTHS[k]
            acc = bank("ssq_acc%d" % k)
            for n in range(w // P):
                for part in range(2):
                    nc.tensor.matmul(
                        out=acc[:, n * P : (n + 1) * P],
                        lhsT=ssq[k][:, 2 * n + part : 2 * n + part + 1].to_broadcast([P, P]), rhs=ident[:],
                        start=(part == 0), stop=(part == 1), is_transpose=True,
                    )
            factor[k] = kept("factor%d" % k, [P, w], F32)
            nc.scalar.activation(
                out=factor[k][:], in_=acc[:, 0:w], func=ACT.Abs_reciprocal_sqrt, scale=1.0 / I, bias=EPS
            )

        out_rows = out.rearrange("(a p) r -> p a r", p=P)

        def make_out(k, a0):
            w = WIDTHS[k]
            tiles = BANK // w
            acc = bank("m_acc%d_%d" % (k, a0))
            for n in range(tiles):
                part, row0 = divmod((a0 + n) * P, PASS)
                rows = slice((a0 + n) * P, (a0 + n + 1) * P)
                for half in range(2):
                    mx(acc[:, n * w : (n + 1) * w],
                       (p_code[part][:, half, row0 : row0 + P], p_scale[PACK * half : P, rows]),
                       (h_mx[k, half][0][:], h_mx[k, half][1][:]), half == 0, half == 1)
            result = kept("result%d_%d" % (k, a0), [P, tiles, w], F32)
            nc.vector.tensor_tensor(
                out=result[:], in0=acc[:].rearrange("p (a r) -> p a r", a=tiles),
                in1=factor[k][:].unsqueeze(1).to_broadcast([P, tiles, w]), op=ALU.mult,
            )
            nc.sync.dma_start(out=out_rows[:, a0 : a0 + tiles, starts[k] : starts[k + 1]], in_=result[:])

        widen_b(0)
        widen_b(1)
        mix_c(0)
        quant_c(0)
        mix_b(0, 0)
        mix_b(0, 1)
        t_code[0] = permute_words("t_code0", t_raw[0])
        quant_b(0)
        q_code[0] = permute_words("q_code0", q_raw[0])
        qt_scale[0] = permute_scales(0)
        qt_scale[1] = permute_scales(1)
        nc.vector.tensor_copy(out=mu_f32[:], in_=mu_raw[:])
        t_code[1] = permute_words("t_code1", t_raw[1])
        mix_c(1, nc.scalar.copy)
        make_f(0)
        mix_b(1, 0)
        q_code[1] = permute_words("q_code1", q_raw[1])
        quant_c(1)
        make_h(0, 0)
        mix_b(1, 1)
        quant_b(1)
        make_h(0, 1)
        make_f(1)
        quant_h(0)
        make_h(1, 0)
        sum_squares(0)
        mix_c(2)
        quant_c(2)

        for k in range(chunks):
            if k + 2 <= last:
                widen_b(k + 2)
            if k + 1 <= last:
                for half in range(1 if k == 0 else 0, 2):
                    make_h(k + 1, half)
            make_factor(k)
            if k + 2 <= last:
                make_f(k + 2)
            if k + 1 <= last:
                quant_h(k + 1)
            between = []
            if k + 2 <= last:
                mix_b(k + 2, 0)
                mix_b(k + 2, 1)
                between.append((quant_b, k + 2))
            if k + 3 <= last:
                between.extend([(mix_c, k + 3), (quant_c, k + 3)])
            firsts = list(range(0, I // P, BANK // WIDTHS[k]))
            sums_after = len(firsts) // 2 if k + 1 == last else len(firsts)
            done = 0
            for n, a0 in enumerate(firsts):
                make_out(k, a0)
                upto = ((n + 1) * len(between) + len(firsts) - 1) // len(firsts)
                for step, chunk in between[done:upto]:
                    step(chunk)
                done = upto
                if n + 1 == sums_after and k + 1 <= last:
                    sum_squares(k + 1)
